import numpy as np
import ml_dtypes


def mxq(x, axis, fmt="e4m3"):
    dtype, down = {"e4m3": (ml_dtypes.float8_e4m3fn, 7), "e5m2": (ml_dtypes.float8_e5m2, 14)}[fmt]
    v = np.moveaxis(np.asarray(x, np.float32).astype(ml_dtypes.bfloat16).astype(np.float64), axis, -1)
    blocks = v.reshape(v.shape[:-1] + (-1, 32))
    amax = np.abs(blocks).max(-1, keepdims=True)
    byte = np.maximum(np.where(amax > 0, np.frexp(amax)[1] - 1 + 127, 0) - down, 1)
    scale = np.exp2(byte - 127.0)
    codes = (blocks / scale).astype(np.float32).astype(dtype).astype(np.float64)
    return np.moveaxis((codes * scale).reshape(v.shape), -1, axis)


WIDE = False


def mx_kscale(k):
    if not WIDE:
        return np.ones(k)
    levels = np.array([10, -10, 5, -5, 0])
    if k % 512:
        return np.exp2(np.random.permutation(np.resize(levels, k // 32))).repeat(32)
    a = np.empty((k // 512, 16))
    for p in range(k // 512):
        a[p, :8] = np.random.permutation(np.resize(levels, 8))
        for g in range(8):
            far = levels[np.abs(levels - a[p, g]) >= 10]
            a[p, g + 8] = far[np.random.randint(len(far))]
    return np.exp2(a.ravel()).repeat(32)


def f64(x):
    return np.asarray(x).astype(np.float64)


def striped(idx):
    return np.tile(idx.reshape(-1, 16).T, (8, 1)).astype(np.uint16)


def unstriped(offs):
    return offs[:16].T.reshape(-1).astype(np.int64)


E2M1 = np.array([0.0, 0.5, 1.0, 1.5, 2.0, 3.0, 4.0, 6.0, -0.0, -0.5, -1.0, -1.5, -2.0, -3.0, -4.0, -6.0])


def pack_weight(w, fmt):
    k, n = w.shape
    w = f64(np.asarray(w, np.float32).astype(ml_dtypes.bfloat16)).reshape(k // 32, 32, n)
    amax = np.abs(w).max(1)
    if fmt == "e4m3":
        byte = np.frexp(amax)[1] - 1 + 127 - 7
    else:
        mant, ex = np.frexp(amax / 6.0)
        byte = np.where(mant > 0.5, ex, ex - 1) + 127
    byte = np.clip(np.where(amax > 0, byte, 1), 1, 254)
    scaled = (w * np.exp2(127.0 - byte)[:, None, :]).reshape(k, n).astype(np.float32)
    by_word = np.ascontiguousarray(scaled.reshape(k // 512, 128, 4, n).transpose(0, 1, 3, 2))
    if fmt == "e4m3":
        words = by_word.astype(ml_dtypes.float8_e4m3fn).view(np.uint8)
    else:
        c = by_word.astype(ml_dtypes.float4_e2m1fn).view(np.uint8) & 0xF
        words = (c[..., 0::2] | (c[..., 1::2] << 4)).reshape(k // 512, 128, 2 * n)
    return np.ascontiguousarray(words), np.ascontiguousarray(byte.astype(np.uint8).reshape(k // 512, 16, n))


def unpack_weight(words, scales, fmt):
    g, _, n = scales.shape
    words = np.ascontiguousarray(words).reshape(g, 128, n, -1)
    if fmt == "e4m3":
        vals = words.view(ml_dtypes.float8_e4m3fn).astype(np.float64)
    else:
        nib = np.empty((g, 128, n, 4), np.uint8)
        nib[..., 0::2] = words & 0xF
        nib[..., 1::2] = words >> 4
        vals = E2M1[nib]
    vals = vals * np.repeat(np.exp2(scales.astype(np.float64) - 127.0), 8, axis=1)[..., None]
    return vals.transpose(0, 1, 3, 2).reshape(g * 512, n)


def gelu(v):
    return 0.5 * v * (1.0 + np.tanh(np.sqrt(2.0 / np.pi) * (v + 0.044715 * v**3)))


K, T, S, H, T2, P, N = 1536, 4096, 1024, 512, 2048, 512, 768

def setup_inputs():
    n = np.random.standard_normal
    s = mx_kscale(K)[:, None]
    u = mx_kscale(H)[:, None]
    tab_words, tab_scales = pack_weight(n((K, T)) * s, "e4m3")
    w1_words, w1_scales = pack_weight(n((K, H)) * 1.5 / np.sqrt(K) / s, "e2m1")
    perm = np.random.permutation(T2)
    return {
        "tab_words": tab_words, "tab_scales": tab_scales,
        "offs": striped(np.random.permutation(T)[:S]),
        "w1_words": w1_words, "w1_scales": w1_scales,
        "gain": (1.2 * np.exp(0.3 * n(H)) * u[:, 0]).astype(np.float32),
        "page0": (n((H, T2)) * u).astype(np.float32),
        "wgs": np.exp(0.3 * n((128, S))).astype(np.float32),
        "offs2": striped(np.random.permutation(T2)[:S]),
        "offs3": striped(perm[:P]),
        "offs4": striped(perm[P:2 * P]),
        "w2": (n((H, N)) / np.sqrt(H) / u).astype(np.float32),
    }

def reference(tab_words, tab_scales, offs, w1_words, w1_scales, gain, page0, wgs, offs2, offs3, offs4, w2):
    v = unpack_weight(tab_words, tab_scales, "e4m3")[:, unstriped(offs)]
    w1 = unpack_weight(w1_words, w1_scales, "e2m1")
    h = np.tanh(w1.T @ v) * f64(gain)[:, None]
    page = f64(page0).copy()
    page[:, unstriped(offs2)] = np.tile(f64(wgs), (H // 128, 1)) * h
    a = page[:, unstriped(offs3)]
    b = page[:, unstriped(offs4)]
    page[:, unstriped(offs3)] = np.sqrt(a * a + b * b)
    page[:, unstriped(offs4)] = np.maximum(a, b)
    out = mxq(f64(w2), 0, "e4m3").T @ mxq(page, 0, "e4m3")
    return out

from contextlib import ExitStack

import concourse.mybir as mybir
from concourse.masks import make_identity

K, T, S, H, T2, PAIRS, N = 1536, 4096, 1024, 512, 2048, 512, 768
FLOPS = 2 * K * H * S + 2 * H * N * T2

F32 = mybir.dt.float32
BF16 = mybir.dt.bfloat16
I32 = mybir.dt.int32
U32 = mybir.dt.uint32
U16 = mybir.dt.uint16
U8 = mybir.dt.uint8
FP8X4 = mybir.dt.float8_e4m3fn_x4
FP4X4 = mybir.dt.float4_e2m1fn_x4
ACT = mybir.ActivationFunctionType
ALU = mybir.AluOpType

P = 128
PACK = 4
PASSES = K // (P * PACK)
BANK = 512
HALVES = S // BANK
CHUNKS = ((0, 256), (256, 512), (512, 1024), (1024, 1536), (1536, 2048))
M_TILES = N // P
SLOT = (0, 2, 1, 3)


def tile_list_repertoire_page_exchange_kernel(
    tc, tab_words, tab_scales, offs, w1_words, w1_scales, gain, page0, wgs, offs2, offs3, offs4, w2, out
):
    nc = tc.nc
    with ExitStack() as ctx:
        lists = ctx.enter_context(tc.tile_pool(name="lists", bufs=1))
        keep = ctx.enter_context(tc.tile_pool(name="keep", bufs=1))
        psum = ctx.enter_context(tc.psum_pool(name="psum", bufs=1))

        banks = [psum.tile([P, BANK], F32, name="bank%d" % i) for i in range(8)]

        def held(shape, dtype, name, tag=None):
            return keep.tile(shape, dtype, name=name, tag=tag or name, align_bytes=64)

        idx = lists.tile([P, S // 16], U16, name="idx")
        idx2 = lists.tile([P, S // 16], U16, name="idx2")
        idx3 = lists.tile([P, PAIRS // 16], U16, name="idx3")
        idx4 = lists.tile([P, PAIRS // 16], U16, name="idx4")

        scale_tables = [held([P, T], U8, "scale_table%d" % i, tag="scale_table%d" % i) for i in range(2)]
        nc.vector.memset(scale_tables[1][:].bitcast(I32), 0)
        w1_scale_raw = held([P, PASSES, H], U8, "w1_scale_raw")
        nc.vector.memset(w1_scale_raw[:].rearrange("p a c -> p (a c)").bitcast(I32), 0)
        nc.vector.memset(scale_tables[0][0:96, :].bitcast(I32), 0)
        picked_scales = held([P, 2 * S], U8, "picked_scales")
        plane_first = held([P, S], U8, "plane_first")
        plane_rest = held([P, 2 * S], U8, "plane_rest")
        v_planes = [plane_first[:], plane_rest[:, 0:S], plane_rest[:, S : 2 * S]]

        nc.sync.dma_start(idx[:], offs)
        scale_rows = tab_scales.rearrange("a q t -> (a q) t").bitcast(I32)
        nc.sync.dma_start(scale_tables[0][96:128, :].bitcast(I32), scale_rows[0:32, :])
        nc.gpsimd.dma_start(scale_tables[1][112:128, :].bitcast(I32), scale_rows[32:48, :])
        for q in range(4):
            nc.gpsimd.dma_start(
                w1_scale_raw[32 * q : 32 * q + 4, :, :].bitcast(I32),
                w1_scales[:, 4 * q : 4 * q + 4, :].rearrange("a r c -> r a c").bitcast(I32),
            )
        nc.gpsimd.memset(plane_first[:].bitcast(I32), 0)
        nc.gpsimd.memset(plane_rest[:].bitcast(I32), 0)
        word_tables = [held([P, T], U32, "word_table%d" % a, tag="big%d" % a) for a in range(PASSES)]
        w1_raw = held([P, PASSES, 2 * H], U8, "w1_raw")

        def load_words(a):
            nc.sync.dma_start(
                word_tables[a][:].bitcast(I32), tab_words[a].rearrange("p t i -> p (t i)").bitcast(I32)
            )

        load_words(0)
        nc.sync.dma_start(w1_raw[:].bitcast(I32), w1_words.rearrange("a p c -> p a c").bitcast(I32))
        load_words(1)
        load_words(2)
        gains = held([P, PACK], F32, "gains")
        nc.sync.dma_start(gains[:], gain.rearrange("(p t) -> p t", t=PACK))

        wgs_rows = wgs.rearrange("(p t) j -> p (t j)", t=PACK)
        page_rows = page0.rearrange("(p t) c -> t p c", t=PACK)
        wg_cuts = (0, BANK, S, 2 * S, PACK * S)
        wg_parts = [held([P, wg_cuts[i + 1] - wg_cuts[i]], F32, "wg%d" % i) for i in range(4)]
        pages = [held([P, T2], F32, "page%d" % t) for t in range(PACK)]

        def load_wg(i):
            for q in (0, 2, 1, 3):
                nc.sync.dma_start(wg_parts[i][32 * q : 32 * q + 32, :], wgs_rows[:, wg_cuts[i] : wg_cuts[i + 1]])

        def wg_cols(t, lo, hi):
            lo, hi = t * S + lo, t * S + hi
            i = max(j for j in range(4) if wg_cuts[j] <= lo)
            return wg_parts[i][:, lo - wg_cuts[i] : hi - wg_cuts[i]]

        load_wg(0)
        nc.sync.dma_start(idx2[:], offs2)
        nc.sync.dma_start(pages[0][:], page_rows[0])
        load_wg(1)
        nc.sync.dma_start(pages[1][:], page_rows[1])
        load_wg(2)
        nc.sync.dma_start(idx3[:], offs3)
        nc.sync.dma_start(idx4[:], offs4)
        nc.sync.dma_start(pages[2][:], page_rows[2])
        load_wg(3)
        nc.sync.dma_start(pages[3][:], page_rows[3])
        w2_raw = held([P, PACK, N], F32, "w2_raw")
        nc.sync.dma_start(w2_raw[:], w2.rearrange("(p j) n -> p j n", j=PACK))

        ident = held([P, P], F32, "ident")
        make_identity(nc, ident[:])

        for i in range(2):
            nc.vector.tensor_copy(picked_scales[:, i * S : (i + 1) * S], scale_tables[i][:].indirect(idx[:]))
        for q in range(4):
            nc.gpsimd.dma_start(
                plane_first[32 * q : 32 * q + 4, :].bitcast(I32),
                picked_scales[96 + 4 * q : 100 + 4 * q, 0:S].bitcast(I32),
            )
        for q in range(4):
            nc.gpsimd.dma_start(
                plane_rest[32 * q : 32 * q + 4, :].bitcast(I32),
                picked_scales[112 + 4 * q : 116 + 4 * q, :].bitcast(I32),
            )

        w1_scale = held([P, PASSES, H], U8, "w1_scale")
        nc.vector.tensor_copy(
            w1_scale[:].rearrange("p a (t m) -> p a t m", t=PACK),
            w1_scale_raw[:].rearrange("p a (m t) -> p a t m", t=PACK),
        )
        w1_codes = held([P, PASSES, 2 * H], U8, "w1_codes", tag="scale_table1")
        nc.vector.tensor_copy(
            w1_codes[:].bitcast(U16).rearrange("p a (t m) -> p a t m", t=PACK),
            w1_raw[:].bitcast(U16).rearrange("p a (m t) -> p a t m", t=PACK),
        )
        picked = []
        for a, tag in enumerate(("w1_raw", "w1_scale_raw")):
            whole = held([P, S], U32, "picked%d" % a, tag=tag)
            nc.vector.tensor_copy(whole[:], word_tables[a][:].indirect(idx[:]))
            picked.append([whole[:, hf * BANK : (hf + 1) * BANK] for hf in range(HALVES)])
        whole = held([P, S], U32, "picked2", tag="big1")
        picked.append([whole[:, hf * BANK : (hf + 1) * BANK] for hf in range(HALVES)])
        for hf in range(HALVES):
            nc.vector.tensor_copy(
                picked[2][hf], word_tables[2][:].indirect(idx[:, hf * BANK // 16 : (hf + 1) * BANK // 16])
            )

        acc = [[banks[HALVES * t + hf] for hf in range(HALVES)] for t in range(PACK)]
        act = [held([P, N * 2 if t == 2 else S], F32, "act%d" % t) for t in range(PACK)]

        def first_pass(a, t, hf):
            cols = slice(hf * BANK, (hf + 1) * BANK)
            nc.tensor.matmul_mx(
                out=acc[t][hf][:],
                lhsT=w1_codes[:, a, 2 * P * t : 2 * P * (t + 1)].bitcast(FP4X4),
                lhsT_scale=w1_scale[:, a, P * t : P * (t + 1)],
                rhs=picked[a][hf].bitcast(FP8X4),
                rhs_scale=v_planes[a][:, cols],
                start=(a == 0),
                stop=(a == PASSES - 1),
            )

        def gained(t, out_ap, in_ap):
            nc.scalar.activation(out_ap, in_ap, ACT.Copy, scale=gains[:, t : t + 1])

        for t in range(PACK):
            for hf in range(HALVES):
                first_pass(0, t, hf)
        first_factor = held([P, BANK], F32, "first_factor")
        gained(0, first_factor[:], wg_cols(0, 0, BANK))
        for t in range(PACK):
            for hf in range(HALVES):
                for a in range(1, PASSES):
                    first_pass(a, t, hf)
                nc.scalar.activation(act[t][:, hf * BANK : (hf + 1) * BANK], acc[t][hf][:], ACT.Tanh)
            if t < PACK - 1:
                rest = act[t][:, BANK if t == 0 else 0 : S]
                gained(t, rest, rest)

        grouped = [held([P, hi - lo, PACK], BF16, "grouped%d" % c) for c, (lo, hi) in enumerate(CHUNKS)]
        lower, upper = slice(0, PAIRS), slice(PAIRS, 2 * PAIRS)
        sides = [[act[1][:, lower], act[1][:, upper]]] + [[first_factor[:], act[3][:, upper]]] * (PACK - 1)
        norms = [act[0][:, upper if t % 2 else lower] for t in range(PACK)]
        larger = [act[2][:, lower]] + norms[: PACK - 1]
        squares = held([P, 2, PAIRS], F32, "squares")

        def put(t, lo, hi, values, factor):
            nc.vector.tensor_tensor(pages[t][:].indirect(idx2[:, lo // 16 : hi // 16]), values, factor, ALU.mult)

        def fetch(t, side):
            nc.vector.tensor_copy(sides[t][side], pages[t][:].indirect((idx3, idx4)[side][:]))
            for c in range(PAIRS // P):
                cols = slice(c * P, (c + 1) * P)
                nc.tensor.transpose(banks[side][:, cols], sides[t][side][:, cols], ident[:])
            nc.scalar.activation(squares[:, side, :], banks[side][:], ACT.Square)
            if side == 1:
                for half in range(2):
                    for i in range(2):
                        c = 2 * half + i
                        for s in range(2):
                            nc.tensor.matmul(
                                banks[half][:, i * P : (i + 1) * P],
                                squares[:, s, c * P : (c + 1) * P],
                                ident[:],
                                start=(s == 0),
                                stop=(s == 1),
                                is_transpose=True,
                            )
                    nc.scalar.activation(
                        norms[t][:, 2 * half * P : 2 * (half + 1) * P], banks[half][:, 0 : 2 * P], ACT.Sqrt
                    )

        def take_max(t):
            nc.vector.tensor_tensor(larger[t], sides[t][0], sides[t][1], ALU.max)

        def put_max(t):
            nc.vector.tensor_copy(pages[t][:].indirect(idx4[:]), larger[t])

        def put_norm(t):
            nc.vector.tensor_copy(pages[t][:].indirect(idx3[:]), norms[t])

        def round_page(t, c, engine_copy):
            engine_copy(grouped[c][:, :, SLOT[t]], pages[t][:, CHUNKS[c][0] : CHUNKS[c][1]])

        def round_on_scalar(t):
            for c in range(len(CHUNKS)):
                round_page(t, c, nc.scalar.copy)

        w2_codes = held([P, N], U32, "w2_codes")
        w2_scale = held([P, N], U8, "w2_scale")

        def quantise_w2():
            w2_grouped = act[2][:].bitcast(BF16).rearrange("p (n j) -> p n j", j=PACK)
            nc.scalar.copy(
                w2_grouped.rearrange("p n (lo hi) -> p n lo hi", lo=2),
                w2_raw[:].rearrange("p (hi lo) n -> p n lo hi", lo=2),
            )
            for i in range(3):
                cols = slice(i * 256, (i + 1) * 256)
                nc.vector.quantize_mx(
                    out=w2_codes[:, cols].bitcast(FP8X4),
                    scales=w2_scale[:, cols],
                    in_=w2_grouped[:, cols, :].rearrange("p n j -> p (n j)"),
                )

        put(0, 0, BANK, act[0][:, 0:BANK], first_factor[:])
        put(0, BANK, S, act[0][:, BANK:S], wg_cols(0, BANK, S))
        put(1, 0, S, act[1][:], wg_cols(1, 0, S))
        fetch(0, 0)
        fetch(0, 1)
        put(2, 0, S, act[2][:, 0:S], wg_cols(2, 0, S))
        for t in range(PACK):
            take_max(t)
            if t + 1 < PACK:
                fetch(t + 1, 0)
            put_max(t)
            if t == 0:
                gained(3, act[1][:], act[3][:])
                put(3, 0, S, act[1][:], wg_cols(3, 0, S))
            if t + 1 < PACK:
                fetch(t + 1, 1)
            put_norm(t)
            if t == 0:
                quantise_w2()
            if t + 1 < PACK:
                round_on_scalar(t)

        out_rows = out.rearrange("(m p) c -> p m c", p=P)
        used = 0
        for c, (lo, hi) in enumerate(CHUNKS):
            width = hi - lo
            round_page(PACK - 1, c, nc.vector.tensor_copy)
            codes = held([P, width], U32, "page_codes%d" % c)
            scales = held([P, width], U8, "page_scale%d" % c)
            nc.vector.quantize_mx(
                out=codes[:].bitcast(FP8X4), scales=scales[:], in_=grouped[c][:].rearrange("p c t -> p (c t)")
            )
            staged = held([P, M_TILES, width], F32, "staged%d" % c, tag="big%d" % c)
            per_bank = BANK // width
            for m0 in range(0, M_TILES, per_bank):
                res = banks[(2 + used) % 8]
                used = used + 1
                for i in range(per_bank):
                    m = m0 + i
                    nc.tensor.matmul_mx(
                        out=res[:, i * width : (i + 1) * width],
                        lhsT=w2_codes[:, m * P : (m + 1) * P].bitcast(FP8X4),
                        lhsT_scale=w2_scale[:, m * P : (m + 1) * P],
                        rhs=codes[:].bitcast(FP8X4),
                        rhs_scale=scales[:],
                        start=True,
                        stop=True,
                    )
                done = m0 + per_bank
                part = staged[:, m0:done, :].rearrange("p m c -> p (m c)")
                if (c >= 3 and m0 % 2 == 1) or (c == 2 and m0 == 5):
                    nc.vector.tensor_copy(part, res[:])
                else:
                    nc.scalar.copy(part, res[:])
                if done % 2 == 0:
                    nc.sync.dma_start(out_rows[:, done - 2 : done, lo:hi], staged[:, done - 2 : done, :])
